import numpy as np, ml_dtypes
CORES = [32,33,34,35,36,37,38,39,40,41,42,43,48,49]
N = 14
G1 = [0,1,2,3,4,5,6,7,8,9,10,11,12,13]
ROOT1 = 11
G2 = [0,1,2,3,4,5,6,7]
G3 = [8,9,10,11,12,13]
ROOT3 = 2
def setup_inputs(rng):
    return {"x1": rng.standard_normal((N, 128, 4), dtype=np.float32), "x2": rng.standard_normal((N, 128, 256), dtype=np.float32).astype(ml_dtypes.bfloat16), "x3": rng.standard_normal((N, 128, 2), dtype=np.float32)}
def reference(x1, x2, x3):
    out = {}
    y = np.full((N, 128, 4), np.nan, x1.dtype)
    for r in G1:
        y[r] = x1[G1[ROOT1]]
    out["y1"] = y
    y = np.full((N, 128, 256), np.nan, x2.dtype)
    for i, r in enumerate(G2):
        y[r] = np.concatenate([x2[s][:, 32 * i:32 * i + 32] for s in G2], axis=1)
    out["y2"] = y
    y = np.full((N, 128, 2), np.nan, x3.dtype)
    y[G3[ROOT3]] = x3[G3].sum(axis=0, dtype=np.float64).astype(x3.dtype)
    out["y3"] = y
    return out

@@ -1,0 +1,114 @@
+from concourse.bass import DstId, RemoteDMATransfer
+from concourse.mybir import AluOpType
+
+SCRATCH = {
+    "snd": ("sbuf", [128, 256], "bfloat16"),
+    "land": ("sbuf", [128, 256], "bfloat16"),
+    "b1": ("dram", [128, 4], "float32"),
+    "s3": ("dram", [128, 2], "float32"),
+    "slot": ("dram", [3, 128, 2], "float32"),
+    "p1": ("dram", [128, 2], "float32"),
+    "p2": ("dram", [128, 2], "float32"),
+}
+SEMAPHORES = ["ld1", "ld2", "ld3", "arr1", "arr2", "arr3", "part1", "part2", "sent", "st1", "st2", "st3", "acc3"]
+
+
+def rank_program(g, core, T, topo):
+    tb = T.tables
+    G1 = [T.cores[r] for r in tb["G1"]]
+    G2 = [T.cores[r] for r in tb["G2"]]
+    G3 = [T.cores[r] for r in tb["G3"]]
+    root1 = G1[tb["ROOT1"]]
+    root3 = G3[tb["ROOT3"]]
+    S = T.sem
+
+    def did(c):
+        rid, pid, _ = topo.addr(c)
+        return DstId(rid=rid, pnc=pid)
+
+    near = [c for c in G3 if topo.chip(c) == topo.chip(root3)]
+    far = [c for c in G3 if topo.chip(c) != topo.chip(root3)]
+    fold_near = [c for c in near if c != root3 and c != root1][0]
+    far_chip = topo.chip(far[0])
+    fold_far = [c for c in range(far_chip * 8, far_chip * 8 + 8)
+                if c not in T.cores and topo.may_write(c, root3)][0]
+    near_send = [c for c in near if c != fold_near]
+
+    two_hop = [c for c in G1 if topo.chip(c) != topo.chip(root1) and not topo.mates(topo.chip(c), topo.chip(root1))]
+    mate = [c for c in G1 if topo.mates(topo.chip(c), topo.chip(root1))]
+    local = [c for c in G1 if topo.chip(c) == topo.chip(root1) and c != root1]
+    bplan = [(two_hop, 0x0003), (mate[:4], 0x000C), (mate[4:], 0x0030), (local, 0x0300)]
+
+    sent = 0
+
+    if core in G3:
+        g.sync.dma_start(T.s3[:], T.x3[:]).then_inc(S.ld3, 16)
+    if core == root1:
+        g.scalar.dma_start(T.b1[:], T.x1[:]).then_inc(S.ld1, 16)
+        g.scalar.dma_start(T.y1[:], T.x1[:]).then_inc(S.st1, 16)
+    if core in G2:
+        me = G2.index(core)
+        g.sync.dma_start(T.snd[:], T.x2[:]).then_inc(S.ld2, 16)
+        g.scalar.dma_start(T.land[:, 32 * me:32 * me + 32], T.x2[:, 32 * me:32 * me + 32]).then_inc(S.arr2, 16)
+
+    if core in near_send or core in far:
+        to, k = (fold_near, near_send.index(core)) if core in near_send else (fold_far, far.index(core))
+        rid, pid, _ = topo.addr(to)
+        g.wait_ge(S.ld3, 16)
+        g.remote_dma(T.slot[k], T.s3[:], S.arr3, S.sent, pid, rid, 0x8000)
+        sent += 1
+
+    if core == root1:
+        g.wait_ge(S.ld1, 16)
+        g.remote_dma_fused(
+            [RemoteDMATransfer(dst_ids=[did(c) for c in ds], dma_engine_mask=m, remote_sem=S.arr1,
+                               srcs=[T.b1[:]], dsts=[T.b1[:] for _ in ds]) for ds, m in bplan if ds],
+            local_sem=S.sent)
+        sent += sum(2 for ds, m in bplan if ds)
+
+    if core in G2:
+        n2 = len(G2)
+        g.wait_ge(S.ld2, 16)
+        trs = []
+        for t in range(n2 - 1):
+            j = (me + 1 + t) % n2
+            trs.append(RemoteDMATransfer(dst_ids=[did(G2[j])], dma_engine_mask=0x3 << (2 * t), remote_sem=S.arr2,
+                                         src=T.snd[:, 32 * j:32 * j + 32], dst=T.land[:, 32 * me:32 * me + 32]))
+        g.remote_dma_fused(trs, local_sem=S.sent)
+        sent += 2 * (n2 - 1)
+
+    if core == fold_near:
+        g.wait_ge(S.ld3, 16)
+        g.wait_ge(S.arr3, len(near_send))
+        g.remote_dma_fused(
+            [RemoteDMATransfer(dst_ids=[did(root3)], dma_engine_mask=0x1, remote_sem=S.part2,
+                               srcs=[T.s3[:]] + [T.slot[k] for k in range(len(near_send))], dsts=[T.p2[:]],
+                               alu_op=1)], local_sem=S.sent)
+        sent += 1
+    if core == fold_far:
+        g.wait_ge(S.arr3, len(far))
+        g.remote_dma_fused(
+            [RemoteDMATransfer(dst_ids=[did(root3)], dma_engine_mask=0x1, remote_sem=S.part1,
+                               srcs=[T.slot[k] for k in range(len(far))], dsts=[T.p1[:]], alu_op=1)],
+            local_sem=S.sent)
+        sent += 1
+
+    if core == root3:
+        g.sync.wait_ge(S.part2, 1)
+        g.sync.dma_start(T.y3[:], T.p2[:]).then_inc(S.st3, 16)
+        g.wait_ge(S.st3, 16)
+        g.wait_ge(S.part1, 1)
+        g.dma_start(T.y3[:], T.p1[:], accum_op=AluOpType.add).then_inc(S.acc3, 16)
+        g.wait_ge(S.acc3, 16)
+
+    if core in G1 and core != root1:
+        g.scalar.wait_ge(S.arr1, 2)
+        g.scalar.dma_start(T.y1[:], T.b1[:]).then_inc(S.st1, 16)
+    if core in G1:
+        g.scalar.wait_ge(S.st1, 16)
+    if core in G2:
+        g.sync.wait_ge(S.arr2, 16 + 2 * (len(G2) - 1))
+        g.sync.dma_start(T.y2[:], T.land[:]).then_inc(S.st2, 16)
+        g.sync.wait_ge(S.st2, 16)
+    if sent:
+        g.wait_ge(S.sent, sent)

@@ -12,6 +12,11 @@ SCRATCH = {
 }
 SEMAPHORES = ["ld1", "ld2", "ld3", "arr1", "arr2", "arr3", "part1", "part2", "sent", "st1", "st2", "st3", "acc3"]
 
+E2 = 2
+E3 = 8
+M3_ON = 0xFF00
+M3_OFF = 0x00FF
+
 
 def rank_program(g, core, T, topo):
     tb = T.tables
@@ -55,8 +60,8 @@ def rank_program(g, core, T, topo):
         to, k = (fold_near, near_send.index(core)) if core in near_send else (fold_far, far.index(core))
         rid, pid, _ = topo.addr(to)
         g.wait_ge(S.ld3, 16)
-        g.remote_dma(T.slot[k], T.s3[:], S.arr3, S.sent, pid, rid, 0x8000)
-        sent += 1
+        g.remote_dma(T.slot[k], T.s3[:], S.arr3, S.sent, pid, rid, M3_ON)
+        sent += E3
 
     if core == root1:
         g.wait_ge(S.ld1, 16)
@@ -72,32 +77,33 @@ def rank_program(g, core, T, topo):
         trs = []
         for t in range(n2 - 1):
             j = (me + 1 + t) % n2
-            trs.append(RemoteDMATransfer(dst_ids=[did(G2[j])], dma_engine_mask=0x3 << (2 * t), remote_sem=S.arr2,
+            trs.append(RemoteDMATransfer(dst_ids=[did(G2[j])], dma_engine_mask=((1 << E2) - 1) << (E2 * t),
+                                         remote_sem=S.arr2,
                                          src=T.snd[:, 32 * j:32 * j + 32], dst=T.land[:, 32 * me:32 * me + 32]))
         g.remote_dma_fused(trs, local_sem=S.sent)
-        sent += 2 * (n2 - 1)
+        sent += E2 * (n2 - 1)
 
     if core == fold_near:
         g.wait_ge(S.ld3, 16)
-        g.wait_ge(S.arr3, len(near_send))
+        g.wait_ge(S.arr3, E3 * len(near_send))
         g.remote_dma_fused(
-            [RemoteDMATransfer(dst_ids=[did(root3)], dma_engine_mask=0x1, remote_sem=S.part2,
+            [RemoteDMATransfer(dst_ids=[did(root3)], dma_engine_mask=M3_ON, remote_sem=S.part2,
                                srcs=[T.s3[:]] + [T.slot[k] for k in range(len(near_send))], dsts=[T.p2[:]],
                                alu_op=1)], local_sem=S.sent)
-        sent += 1
+        sent += E3
     if core == fold_far:
-        g.wait_ge(S.arr3, len(far))
+        g.wait_ge(S.arr3, E3 * len(far))
         g.remote_dma_fused(
-            [RemoteDMATransfer(dst_ids=[did(root3)], dma_engine_mask=0x1, remote_sem=S.part1,
+            [RemoteDMATransfer(dst_ids=[did(root3)], dma_engine_mask=M3_OFF, remote_sem=S.part1,
                                srcs=[T.slot[k] for k in range(len(far))], dsts=[T.p1[:]], alu_op=1)],
             local_sem=S.sent)
-        sent += 1
+        sent += E3
 
     if core == root3:
-        g.sync.wait_ge(S.part2, 1)
+        g.sync.wait_ge(S.part2, E3)
         g.sync.dma_start(T.y3[:], T.p2[:]).then_inc(S.st3, 16)
         g.wait_ge(S.st3, 16)
-        g.wait_ge(S.part1, 1)
+        g.wait_ge(S.part1, E3)
         g.dma_start(T.y3[:], T.p1[:], accum_op=AluOpType.add).then_inc(S.acc3, 16)
         g.wait_ge(S.acc3, 16)
 
@@ -107,7 +113,7 @@ def rank_program(g, core, T, topo):
     if core in G1:
         g.scalar.wait_ge(S.st1, 16)
     if core in G2:
-        g.sync.wait_ge(S.arr2, 16 + 2 * (len(G2) - 1))
+        g.sync.wait_ge(S.arr2, 16 + E2 * (len(G2) - 1))
         g.sync.dma_start(T.y2[:], T.land[:]).then_inc(S.st2, 16)
         g.sync.wait_ge(S.st2, 16)
     if sent:

from concourse.bass import DstId, RemoteDMATransfer
from concourse.mybir import AluOpType

SCRATCH = {
    "snd": ("sbuf", [128, 256], "bfloat16"),
    "land": ("sbuf", [128, 256], "bfloat16"),
    "b1": ("dram", [128, 4], "float32"),
    "s3": ("dram", [128, 2], "float32"),
    "slot": ("dram", [3, 128, 2], "float32"),
    "p1": ("dram", [128, 2], "float32"),
    "p2": ("dram", [128, 2], "float32"),
}
SEMAPHORES = ["ld1", "ld2", "ld3", "arr1", "arr2", "arr3", "part1", "part2", "sent", "st1", "st2", "st3", "acc3"]

E2 = 2
E3 = 8
M3_ON = 0xFF00
M3_OFF = 0x00FF


def rank_program(g, core, T, topo):
    tb = T.tables
    G1 = [T.cores[r] for r in tb["G1"]]
    G2 = [T.cores[r] for r in tb["G2"]]
    G3 = [T.cores[r] for r in tb["G3"]]
    root1 = G1[tb["ROOT1"]]
    root3 = G3[tb["ROOT3"]]
    S = T.sem

    def did(c):
        rid, pid, _ = topo.addr(c)
        return DstId(rid=rid, pnc=pid)

    near = [c for c in G3 if topo.chip(c) == topo.chip(root3)]
    far = [c for c in G3 if topo.chip(c) != topo.chip(root3)]
    fold_near = [c for c in near if c != root3 and c != root1][0]
    far_chip = topo.chip(far[0])
    fold_far = [c for c in range(far_chip * 8, far_chip * 8 + 8)
                if c not in T.cores and topo.may_write(c, root3)][0]
    near_send = [c for c in near if c != fold_near]

    two_hop = [c for c in G1 if topo.chip(c) != topo.chip(root1) and not topo.mates(topo.chip(c), topo.chip(root1))]
    mate = [c for c in G1 if topo.mates(topo.chip(c), topo.chip(root1))]
    local = [c for c in G1 if topo.chip(c) == topo.chip(root1) and c != root1]
    bplan = [(two_hop, 0x0003), (mate[:4], 0x000C), (mate[4:], 0x0030), (local, 0x0300)]

    sent = 0

    if core in G3:
        g.sync.dma_start(T.s3[:], T.x3[:]).then_inc(S.ld3, 16)
    if core == root1:
        g.scalar.dma_start(T.b1[:], T.x1[:]).then_inc(S.ld1, 16)
        g.scalar.dma_start(T.y1[:], T.x1[:]).then_inc(S.st1, 16)
    if core in G2:
        me = G2.index(core)
        g.sync.dma_start(T.snd[:], T.x2[:]).then_inc(S.ld2, 16)
        g.scalar.dma_start(T.land[:, 32 * me:32 * me + 32], T.x2[:, 32 * me:32 * me + 32]).then_inc(S.arr2, 16)

    if core in near_send or core in far:
        to, k = (fold_near, near_send.index(core)) if core in near_send else (fold_far, far.index(core))
        rid, pid, _ = topo.addr(to)
        g.wait_ge(S.ld3, 16)
        g.remote_dma(T.slot[k], T.s3[:], S.arr3, S.sent, pid, rid, M3_ON)
        sent += E3

    if core == root1:
        g.wait_ge(S.ld1, 16)
        g.remote_dma_fused(
            [RemoteDMATransfer(dst_ids=[did(c) for c in ds], dma_engine_mask=m, remote_sem=S.arr1,
                               srcs=[T.b1[:]], dsts=[T.b1[:] for _ in ds]) for ds, m in bplan if ds],
            local_sem=S.sent)
        sent += sum(2 for ds, m in bplan if ds)

    if core in G2:
        n2 = len(G2)
        g.wait_ge(S.ld2, 16)
        trs = []
        for t in range(n2 - 1):
            j = (me + 1 + t) % n2
            trs.append(RemoteDMATransfer(dst_ids=[did(G2[j])], dma_engine_mask=((1 << E2) - 1) << (E2 * t),
                                         remote_sem=S.arr2,
                                         src=T.snd[:, 32 * j:32 * j + 32], dst=T.land[:, 32 * me:32 * me + 32]))
        g.remote_dma_fused(trs, local_sem=S.sent)
        sent += E2 * (n2 - 1)

    if core == fold_near:
        g.wait_ge(S.ld3, 16)
        g.wait_ge(S.arr3, E3 * len(near_send))
        g.remote_dma_fused(
            [RemoteDMATransfer(dst_ids=[did(root3)], dma_engine_mask=M3_ON, remote_sem=S.part2,
                               srcs=[T.s3[:]] + [T.slot[k] for k in range(len(near_send))], dsts=[T.p2[:]],
                               alu_op=1)], local_sem=S.sent)
        sent += E3
    if core == fold_far:
        g.wait_ge(S.arr3, E3 * len(far))
        g.remote_dma_fused(
            [RemoteDMATransfer(dst_ids=[did(root3)], dma_engine_mask=M3_OFF, remote_sem=S.part1,
                               srcs=[T.slot[k] for k in range(len(far))], dsts=[T.p1[:]], alu_op=1)],
            local_sem=S.sent)
        sent += E3

    if core == root3:
        g.sync.wait_ge(S.part2, E3)
        g.sync.dma_start(T.y3[:], T.p2[:]).then_inc(S.st3, 16)
        g.wait_ge(S.st3, 16)
        g.wait_ge(S.part1, E3)
        g.dma_start(T.y3[:], T.p1[:], accum_op=AluOpType.add).then_inc(S.acc3, 16)
        g.wait_ge(S.acc3, 16)

    if core in G1 and core != root1:
        g.scalar.wait_ge(S.arr1, 2)
        g.scalar.dma_start(T.y1[:], T.b1[:]).then_inc(S.st1, 16)
    if core in G1:
        g.scalar.wait_ge(S.st1, 16)
    if core in G2:
        g.sync.wait_ge(S.arr2, 16 + E2 * (len(G2) - 1))
        g.sync.dma_start(T.y2[:], T.land[:]).then_inc(S.st2, 16)
        g.sync.wait_ge(S.st2, 16)
    if sent:
        g.wait_ge(S.sent, sent)
